import numpy as np
import ml_dtypes


def mxq(x, axis, fmt="e4m3"):
    dtype, down = {"e4m3": (ml_dtypes.float8_e4m3fn, 7), "e5m2": (ml_dtypes.float8_e5m2, 14)}[fmt]
    v = np.moveaxis(np.asarray(x, np.float32).astype(ml_dtypes.bfloat16).astype(np.float64), axis, -1)
    blocks = v.reshape(v.shape[:-1] + (-1, 32))
    amax = np.abs(blocks).max(-1, keepdims=True)
    byte = np.maximum(np.where(amax > 0, np.frexp(amax)[1] - 1 + 127, 0) - down, 1)
    scale = np.exp2(byte - 127.0)
    codes = (blocks / scale).astype(np.float32).astype(dtype).astype(np.float64)
    return np.moveaxis((codes * scale).reshape(v.shape), -1, axis)


WIDE = False


def mx_kscale(k):
    if not WIDE:
        return np.ones(k)
    levels = np.array([10, -10, 5, -5, 0])
    if k % 512:
        return np.exp2(np.random.permutation(np.resize(levels, k // 32))).repeat(32)
    a = np.empty((k // 512, 16))
    for p in range(k // 512):
        a[p, :8] = np.random.permutation(np.resize(levels, 8))
        for g in range(8):
            far = levels[np.abs(levels - a[p, g]) >= 10]
            a[p, g + 8] = far[np.random.randint(len(far))]
    return np.exp2(a.ravel()).repeat(32)


def f64(x):
    return np.asarray(x).astype(np.float64)


def striped(idx):
    return np.tile(idx.reshape(-1, 16).T, (8, 1)).astype(np.uint16)


def unstriped(offs):
    return offs[:16].T.reshape(-1).astype(np.int64)


def striped8(idx):
    return np.concatenate([x.reshape(-1, 16).T for x in idx]).astype(np.uint16)


def runs(offs, k):
    lists = np.stack([offs[16 * r : 16 * r + 16].T.reshape(-1) for r in range(8)]).astype(np.int64)
    return lists[np.arange(k) % 512 // 64]


def pack_weight(w):
    k, n = w.shape
    w = f64(np.asarray(w, np.float32).astype(ml_dtypes.bfloat16)).reshape(k // 32, 32, n)
    amax = np.abs(w).max(1)
    byte = np.clip(np.where(amax > 0, np.frexp(amax)[1] - 1 + 127 - 7, 1), 1, 254)
    scaled = (w * np.exp2(127.0 - byte)[:, None, :]).reshape(k, n).astype(np.float32)
    words = np.ascontiguousarray(scaled.reshape(k // 512, 128, 4, n).transpose(0, 1, 3, 2)).astype(ml_dtypes.float8_e4m3fn).view(np.uint8)
    return words, np.ascontiguousarray(byte.astype(np.uint8).reshape(k // 512, 16, n))


def unpack_weight(words, scales):
    g, p, n, _ = words.shape
    vals = np.ascontiguousarray(words).view(ml_dtypes.float8_e4m3fn).astype(np.float64) * np.repeat(np.exp2(scales.astype(np.float64) - 127.0), 8, axis=1)[..., None]
    return vals.transpose(0, 1, 3, 2).reshape(g * 512, n)


def sigmoid(v):
    return 1.0 / (1.0 + np.exp(-np.maximum(v, -700.0)))

def planes(y):
    n, m = y.shape
    v = y.astype(np.float32).astype(ml_dtypes.bfloat16).astype(np.float64).reshape(n // 32, 32, m)
    top = np.abs(v).max(1)
    byte = np.clip(np.where(top > 0, np.frexp(top)[1] - 1 + 127 - 7, 1), 1, 254)
    codes = (v * np.exp2(127.0 - byte)[:, None, :]).reshape(n, m).astype(np.float32).astype(ml_dtypes.float8_e4m3fn).view(np.uint8)
    words = codes.reshape(n // 512, 128, 4, m).transpose(0, 1, 3, 2)
    return np.ascontiguousarray(words), np.ascontiguousarray(byte.astype(np.uint8).reshape(n // 512, 16, m))


K, T, S, N, H = 512, 2048, 512, 512, 512


def setup_inputs():
    n = np.random.standard_normal
    s = mx_kscale(K)[:, None]
    u = mx_kscale(H)
    packed_xT = pack_weight(n((K, T)) * s)
    packed_w1 = pack_weight(n((K, H)) / np.sqrt(K) / s)
    packed_w2 = pack_weight(n((K, H)) / np.sqrt(K) / s)
    packed_w3 = pack_weight(n((H, N)) / np.sqrt(H) / u[:, None])
    return {
        "x_words": packed_xT[0],
        "x_scales": packed_xT[1],
        "w1_words": packed_w1[0],
        "w1_scales": packed_w1[1],
        "w2_words": packed_w2[0],
        "w2_scales": packed_w2[1],
        "gn": (np.random.uniform(0.5, 1.5, (H, 1)) * u[:, None]).astype(np.float32),
        "w3_words": packed_w3[0],
        "w3_scales": packed_w3[1],
        "offs": striped(np.random.permutation(T)[:S]),
        "two": striped(np.random.permutation(T)[:S]),
        "own_l": striped8(np.stack([np.random.permutation(S) for _ in range(8)])),
        "foe": striped8(np.stack([np.random.permutation(S) for _ in range(8)])),
        "food": striped8(np.stack([np.random.permutation(S) for _ in range(8)])),
    }


def reference(x_words, x_scales, w1_words, w1_scales, w2_words, w2_scales, gn, w3_words, w3_scales, offs, two, own_l, foe, food):
    xq = unpack_weight(x_words, x_scales)[:, unstriped(offs)]
    y = sigmoid(unpack_weight(w1_words, w1_scales).T @ xq)
    x_two = unpack_weight(x_words, x_scales)[:, unstriped(two)]
    c = sigmoid(unpack_weight(w2_words, w2_scales).T @ x_two)
    z = f64(gn) * (y * (0.5 * (y[np.arange(H)[:, None], runs(own_l, H)]) - (c[np.arange(H)[:, None], runs(foe, H)]) + 1.5 * (y * (c[np.arange(H)[:, None], runs(food, H)]))))
    out_0 = unpack_weight(w3_words, w3_scales).T @ mxq(z, 0, "e4m3")
    return (out_0,) + planes(out_0)

@@ -1,0 +1,202 @@
+from contextlib import ExitStack
+
+import concourse.mybir as mybir
+
+K, T, S, N, H = 512, 2048, 512, 512, 512
+FLOPS = 2 * K * H * S * 2 + 2 * H * N * S
+
+F32 = mybir.dt.float32
+BF16 = mybir.dt.bfloat16
+I32 = mybir.dt.int32
+U32 = mybir.dt.uint32
+U16 = mybir.dt.uint16
+U8 = mybir.dt.uint8
+FP8X4 = mybir.dt.float8_e4m3fn_x4
+ALU = mybir.AluOpType
+ACT = mybir.ActivationFunctionType
+
+P = 128
+PACK = 4
+BLOCK = 128
+RING = 4
+CHUNKS = (128, 256, 128)
+LC_ON_SCALAR = (0,)
+GY_ON_SCALAR = (2, 3)
+CAST_ON_SCALAR = (0, 1, 2)
+OUT_AFTER_TILE = 1
+
+
+def tile_picked_foodweb_none_po_kernel(
+    tc, x_words, x_scales, w1_words, w1_scales, w2_words, w2_scales, gn, w3_words, w3_scales,
+    offs, two, own_l, foe, food, out_0, out_1, out_2,
+):
+    nc = tc.nc
+    with ExitStack() as ctx:
+        sb = ctx.enter_context(tc.tile_pool(name="sb", bufs=1))
+        psum = ctx.enter_context(tc.psum_pool(name="psum", bufs=1))
+
+        def load_list(name, src):
+            t = sb.tile([P, S // 16], U16, name=name)
+            nc.sync.dma_start(t[:], src)
+            return t
+
+        def load_words(name, src, width):
+            t = sb.tile([P, width], U32, name=name, align_bytes=64)
+            nc.sync.dma_start(t[:].bitcast(I32), src[0].rearrange("p n t -> p (n t)").bitcast(I32))
+            return t
+
+        def load_scales(dst, src, first=0, quads=range(4)):
+            for q in quads:
+                r = 32 * q + first
+                nc.sync.dma_start(dst[r : r + 4, :].bitcast(I32), src[0][4 * q : 4 * q + 4, :].bitcast(I32))
+
+        def deal_words(name, words):
+            dw = sb.tile([P, H], I32, name=name, align_bytes=64)
+            nc.vector.tensor_copy(
+                out=dw[:].rearrange("p (t c i) -> p c t i", t=PACK, i=4),
+                in_=words[:].bitcast(I32).rearrange("p (c i t) -> p c t i", t=PACK, i=4),
+            )
+            return dw
+
+        def deal_scales(name, scales):
+            ds = sb.tile([P, H], U8, name=name, align_bytes=64)
+            nc.vector.tensor_copy(
+                out=ds[:].rearrange("p (t c i) -> p c t i", t=PACK, i=16),
+                in_=scales[:].rearrange("p (c i t) -> p c t i", t=PACK, i=16),
+            )
+            return ds
+
+        def product(bank, dw, ds, first, t, words, scales):
+            cols = slice(P * t, P * (t + 1))
+            nc.tensor.matmul_mx(
+                out=bank, lhsT=dw[:, cols].bitcast(FP8X4), lhsT_scale=ds[first:P, cols],
+                rhs=words.bitcast(FP8X4), rhs_scale=scales, start=True, stop=True,
+            )
+
+        xs = sb.tile([P, T], U8, name="xs", align_bytes=64)
+        nc.vector.memset(xs[:].bitcast(I32), 0)
+        w12s = sb.tile([P, H], U8, name="w12s", align_bytes=64)
+        w3s = sb.tile([P, N], U8, name="w3s", align_bytes=64)
+        zs = sb.tile([P, S], U8, name="zs", align_bytes=64)
+        for t_ in (w12s, w3s, zs):
+            nc.vector.memset(t_[:].bitcast(I32), 0)
+
+        warm = sb.tile([P, 2], F32, name="warm")
+        nc.vector.memset(warm[:, 0:1], 0.0)
+        nc.scalar.activation(warm[:, 1:2], warm[:, 0:1], ACT.Sigmoid)
+
+        two_t = load_list("two_t", two)
+        offs_t = load_list("offs_t", offs)
+        w2w = load_words("w2w", w2_words, H)
+        load_scales(xs, x_scales)
+        load_scales(w12s, w2_scales, 0, range(0, 1))
+        xw = load_words("xw", x_words, T)
+        load_scales(w12s, w2_scales, 0, range(1, 4))
+        load_scales(w12s, w1_scales, 4)
+        w1w = load_words("w1w", w1_words, H)
+        food_t = load_list("food_t", food)
+        foe_t = load_list("foe_t", foe)
+        g = sb.tile([P, PACK], F32, name="g")
+        nc.sync.dma_start(g[:], gn.rearrange("(p t) o -> p (t o)", t=PACK))
+        own_t = load_list("own_t", own_l)
+        w3w = load_words("w3w", w3_words, N)
+        load_scales(w3s, w3_scales)
+
+        xs2 = sb.tile([P, S], U8, name="xs2", align_bytes=64)
+        nc.vector.tensor_copy(xs2[:], xs[:].indirect(two_t[:]))
+        xs1 = sb.tile([P, S], U8, name="xs1", align_bytes=64)
+        nc.vector.tensor_copy(xs1[:], xs[:].indirect(offs_t[:]))
+        dw2 = deal_words("dw2", w2w)
+        xw2 = sb.tile([P, S], U32, name="xw2", align_bytes=64)
+        nc.vector.tensor_copy(xw2[:], xw[:].indirect(two_t[:]))
+        ds12 = deal_scales("ds12", w12s)
+        pc = [psum.tile([P, S], F32, name=f"pc{t}", tag=f"bank{t}") for t in range(PACK)]
+        for t in range(PACK):
+            product(pc[t][:], dw2, ds12, 0, t, xw2[:], xs2[:])
+        xw1 = sb.tile([P, S], U32, name="xw1", align_bytes=64)
+        nc.vector.tensor_copy(xw1[:], xw[:].indirect(offs_t[:]))
+        dw1 = deal_words("dw1", w1w)
+        py = [psum.tile([P, S], F32, name=f"py{t}", tag=f"bank{PACK + t}") for t in range(PACK)]
+        for t in range(PACK):
+            product(py[t][:], dw1, ds12, 4, t, xw1[:], xs1[:])
+
+        half_g = sb.tile([P, PACK], F32, name="half_g")
+        nc.scalar.activation(half_g[:], g[:], ACT.Copy, scale=0.5)
+
+        lc = [sb.tile([P, S], F32, name=f"lc{t}") for t in range(PACK)]
+        y = [sb.tile([P, S], F32, name=f"y{t}") for t in range(PACK)]
+        gy = sb.tile([P, PACK, S], F32, name="gy")
+        osc = sb.tile([P, S], U8, name="osc", align_bytes=64)
+        ow = sb.tile([P, S], U32, name="ow", align_bytes=64)
+        zw = sb.tile([P, S], U32, name="zw", align_bytes=64)
+        out_rows = out_0.rearrange("(p t) j -> p t j", t=PACK)
+        out_words = out_1[0].rearrange("p n t -> p (n t)").bitcast(I32)
+        w3 = []
+
+        def finish(start, cw):
+            for b0 in range(start, start + cw, BLOCK):
+                b = b0 // BLOCK
+                bcols = slice(b0, b0 + BLOCK)
+                po = psum.tile([P, PACK, BLOCK], F32, name=f"po{b}", tag=f"bank{b}")
+                for t in range(PACK):
+                    product(po[:, t, :], w3[0], w3[1], 0, t, zw[:, bcols], zs[:, bcols])
+                res = sb.tile([P, PACK, BLOCK], F32, name=f"res{b}")
+                rb = sb.tile([P, BLOCK * PACK], BF16, name=f"rb{b}", align_bytes=64)
+                nc.scalar.copy(res[:], po[:])
+                nc.sync.dma_start(out_rows[:, :, bcols], res[:])
+                if b in CAST_ON_SCALAR:
+                    nc.scalar.copy(rb[:].rearrange("p (j t) -> p j t", t=PACK), po[:].rearrange("p t j -> p j t"))
+                else:
+                    nc.vector.tensor_copy(
+                        out=rb[:].rearrange("p (c i t) -> p c t i", t=PACK, i=2),
+                        in_=res[:].rearrange("p t (c i) -> p c t i", i=2),
+                    )
+                nc.vector.quantize_mx(out=ow[:, bcols].bitcast(FP8X4), scales=osc[:, bcols], in_=rb[:])
+                nc.sync.dma_start(out_words[:, bcols], ow[:, bcols].bitcast(I32))
+
+        start = 0
+        pending = None
+        for ci, cw in enumerate(CHUNKS):
+            cols = slice(start, start + cw)
+            lcols = slice(start // 16, (start + cw) // 16)
+            c_food = [sb.tile([P, cw], F32, name=f"c_food{ci}_{t}", tag="c_food", bufs=RING) for t in range(PACK)]
+            c_foe = [sb.tile([P, cw], F32, name=f"c_foe{ci}_{t}", tag="c_foe", bufs=RING) for t in range(PACK)]
+            t1 = sb.tile([P, PACK, cw], F32, name=f"t1_{ci}")
+            t2 = sb.tile([P, PACK, cw], F32, name=f"t2_{ci}")
+            t3 = sb.tile([P, PACK, cw], F32, name=f"t3_{ci}")
+            for t in range(PACK):
+                if ci == 0 and t in LC_ON_SCALAR:
+                    nc.scalar.copy(lc[t][:], pc[t][:])
+                if ci == 0 and t == 0:
+                    for u in range(PACK):
+                        if u not in LC_ON_SCALAR:
+                            nc.vector.tensor_copy(lc[u][:], pc[u][:])
+                nc.scalar.activation(c_food[t][:], lc[t][:].indirect(food_t[:, lcols]), ACT.Sigmoid)
+                if ci == 0:
+                    nc.scalar.activation(y[t][:], py[t][:], ACT.Sigmoid)
+                nc.scalar.activation(c_foe[t][:], lc[t][:].indirect(foe_t[:, lcols]), ACT.Sigmoid)
+                nc.vector.scalar_tensor_tensor(t1[:, t, :], c_food[t][:], 3.0, y[t][:, cols], ALU.mult, ALU.mult)
+                nc.vector.scalar_tensor_tensor(t2[:, t, :], c_foe[t][:], -2.0, t1[:, t, :], ALU.mult, ALU.add)
+                nc.vector.tensor_tensor(t3[:, t, :], y[t][:].indirect(own_t[:, lcols]), t2[:, t, :], ALU.add)
+                if ci == 0 and t in GY_ON_SCALAR:
+                    nc.scalar.activation(gy[:, t, :], y[t][:], ACT.Copy, scale=half_g[:, t : t + 1])
+                elif ci == 0:
+                    nc.vector.tensor_scalar(gy[:, t, :], y[t][:], half_g[:, t : t + 1], None, ALU.mult)
+                if ci == 0 and t == 0:
+                    w3.extend([deal_words("dw3", w3w), deal_scales("ds3", w3s)])
+                if pending is not None and t == OUT_AFTER_TILE:
+                    finish(*pending)
+            zb = sb.tile([P, cw * PACK], BF16, name=f"zb{ci}", align_bytes=64)
+            nc.vector.tensor_tensor(
+                zb[:].rearrange("p (c i t) -> p c t i", t=PACK, i=2),
+                t3[:].rearrange("p t (c i) -> p c t i", i=2),
+                gy[:, :, cols].rearrange("p t (c i) -> p c t i", i=2),
+                ALU.mult,
+            )
+            nc.vector.quantize_mx(out=zw[:, cols].bitcast(FP8X4), scales=zs[:, cols], in_=zb[:])
+            pending = (start, cw)
+            start += cw
+        finish(*pending)
+        for q in range(4):
+            eng = nc.sync if q % 2 == 0 else nc.scalar
+            eng.dma_start(out_2[0][4 * q : 4 * q + 4, :].bitcast(I32), osc[32 * q : 32 * q + 4, :].bitcast(I32))

@@ -17,13 +17,13 @@ ACT = mybir.ActivationFunctionType
 
 P = 128
 PACK = 4
-BLOCK = 128
-RING = 4
-CHUNKS = (128, 256, 128)
+PIECES = ((128, 128), (64, 64, 64, 64))
+HALF = S // 2
+RING = 3
+CHUNKS = (256, 256)
 LC_ON_SCALAR = (0,)
-GY_ON_SCALAR = (2, 3)
 CAST_ON_SCALAR = (0, 1, 2)
-OUT_AFTER_TILE = 1
+OUT_AFTER_TILE = 3
 
 
 def tile_picked_foodweb_none_po_kernel(
@@ -75,25 +75,25 @@ def tile_picked_foodweb_none_po_kernel(
 
         xs = sb.tile([P, T], U8, name="xs", align_bytes=64)
         nc.vector.memset(xs[:].bitcast(I32), 0)
-        w12s = sb.tile([P, H], U8, name="w12s", align_bytes=64)
+        w12s = sb.tile([P, H], U8, name="w12s", tag="raw_then_picked", align_bytes=64)
         w3s = sb.tile([P, N], U8, name="w3s", align_bytes=64)
         zs = sb.tile([P, S], U8, name="zs", align_bytes=64)
-        for t_ in (w12s, w3s, zs):
+        for t_ in (w12s, w3s):
             nc.vector.memset(t_[:].bitcast(I32), 0)
 
         warm = sb.tile([P, 2], F32, name="warm")
         nc.vector.memset(warm[:, 0:1], 0.0)
         nc.scalar.activation(warm[:, 1:2], warm[:, 0:1], ACT.Sigmoid)
 
-        two_t = load_list("two_t", two)
         offs_t = load_list("offs_t", offs)
+        two_t = load_list("two_t", two)
+        w1w = load_words("w1w", w1_words, H)
         w2w = load_words("w2w", w2_words, H)
         load_scales(xs, x_scales)
-        load_scales(w12s, w2_scales, 0, range(0, 1))
+        load_scales(w12s, w1_scales, 0, range(0, 1))
         xw = load_words("xw", x_words, T)
-        load_scales(w12s, w2_scales, 0, range(1, 4))
-        load_scales(w12s, w1_scales, 4)
-        w1w = load_words("w1w", w1_words, H)
+        load_scales(w12s, w1_scales, 0, range(1, 4))
+        load_scales(w12s, w2_scales, 4)
         food_t = load_list("food_t", food)
         foe_t = load_list("foe_t", foe)
         g = sb.tile([P, PACK], F32, name="g")
@@ -102,29 +102,32 @@ def tile_picked_foodweb_none_po_kernel(
         w3w = load_words("w3w", w3_words, N)
         load_scales(w3s, w3_scales)
 
-        xs2 = sb.tile([P, S], U8, name="xs2", align_bytes=64)
-        nc.vector.tensor_copy(xs2[:], xs[:].indirect(two_t[:]))
+        dw1 = deal_words("dw1", w1w)
+        dw2 = deal_words("dw2", w2w)
         xs1 = sb.tile([P, S], U8, name="xs1", align_bytes=64)
         nc.vector.tensor_copy(xs1[:], xs[:].indirect(offs_t[:]))
-        dw2 = deal_words("dw2", w2w)
-        xw2 = sb.tile([P, S], U32, name="xw2", align_bytes=64)
-        nc.vector.tensor_copy(xw2[:], xw[:].indirect(two_t[:]))
+        xs2 = sb.tile([P, S], U8, name="xs2", align_bytes=64)
+        nc.vector.tensor_copy(xs2[:], xs[:].indirect(two_t[:]))
+        y = [sb.tile([P, S], F32, name=f"y{t}") for t in range(PACK)]
+        py = [psum.tile([P, S], F32, name=f"py{t}", tag=f"bank{t}") for t in range(PACK)]
+        xw1_first = sb.tile([P, HALF], U32, name="xw1_first", align_bytes=64)
+        nc.vector.tensor_copy(xw1_first[:], xw[:].indirect(offs_t[:, : HALF // 16]))
         ds12 = deal_scales("ds12", w12s)
-        pc = [psum.tile([P, S], F32, name=f"pc{t}", tag=f"bank{t}") for t in range(PACK)]
+        later = sb.tile([P, HALF + S], U32, name="later", tag="raw_then_picked", align_bytes=64)
+        nc.vector.tensor_copy(later[:, :HALF], xw[:].indirect(offs_t[:, HALF // 16 :]))
+        for a, xw1 in enumerate((xw1_first[:], later[:, :HALF])):
+            hc = slice(a * HALF, (a + 1) * HALF)
+            for t in range(PACK):
+                product(py[t][:, hc], dw1, ds12, 0, t, xw1, xs1[:, hc])
+            for t in range(PACK):
+                nc.scalar.activation(y[t][:, hc], py[t][:, hc], ACT.Sigmoid)
+        xw2 = later[:, HALF:]
+        nc.vector.tensor_copy(xw2, xw[:].indirect(two_t[:]))
+        pc = [psum.tile([P, S], F32, name=f"pc{t}", tag=f"bank{PACK + t}") for t in range(PACK)]
         for t in range(PACK):
-            product(pc[t][:], dw2, ds12, 0, t, xw2[:], xs2[:])
-        xw1 = sb.tile([P, S], U32, name="xw1", align_bytes=64)
-        nc.vector.tensor_copy(xw1[:], xw[:].indirect(offs_t[:]))
-        dw1 = deal_words("dw1", w1w)
-        py = [psum.tile([P, S], F32, name=f"py{t}", tag=f"bank{PACK + t}") for t in range(PACK)]
-        for t in range(PACK):
-            product(py[t][:], dw1, ds12, 4, t, xw1[:], xs1[:])
-
-        half_g = sb.tile([P, PACK], F32, name="half_g")
-        nc.scalar.activation(half_g[:], g[:], ACT.Copy, scale=0.5)
+            product(pc[t][:], dw2, ds12, 4, t, xw2, xs2[:])
 
         lc = [sb.tile([P, S], F32, name=f"lc{t}") for t in range(PACK)]
-        y = [sb.tile([P, S], F32, name=f"y{t}") for t in range(PACK)]
         gy = sb.tile([P, PACK, S], F32, name="gy")
         osc = sb.tile([P, S], U8, name="osc", align_bytes=64)
         ow = sb.tile([P, S], U32, name="ow", align_bytes=64)
@@ -132,30 +135,41 @@ def tile_picked_foodweb_none_po_kernel(
         out_rows = out_0.rearrange("(p t) j -> p t j", t=PACK)
         out_words = out_1[0].rearrange("p n t -> p (n t)").bitcast(I32)
         w3 = []
+        for t in range(PACK):
+            nc.vector.tensor_scalar(gy[:, t, :], y[t][:], g[:, t : t + 1], 0.5, ALU.mult, ALU.mult)
 
-        def finish(start, cw):
-            for b0 in range(start, start + cw, BLOCK):
-                b = b0 // BLOCK
-                bcols = slice(b0, b0 + BLOCK)
-                po = psum.tile([P, PACK, BLOCK], F32, name=f"po{b}", tag=f"bank{b}")
+        res = sb.tile([P, PACK, S], F32, name="res")
+        rbs = {}
+
+        def finish(pieces):
+            for b, c0, w in pieces:
+                bcols = slice(c0, c0 + w)
+                po = psum.tile([P, PACK, w], F32, name=f"po{b}", tag=f"bank{b % PACK}")
                 for t in range(PACK):
                     product(po[:, t, :], w3[0], w3[1], 0, t, zw[:, bcols], zs[:, bcols])
-                res = sb.tile([P, PACK, BLOCK], F32, name=f"res{b}")
-                rb = sb.tile([P, BLOCK * PACK], BF16, name=f"rb{b}", align_bytes=64)
-                nc.scalar.copy(res[:], po[:])
-                nc.sync.dma_start(out_rows[:, :, bcols], res[:])
+                rbs[b] = sb.tile([P, w * PACK], BF16, name=f"rb{b}", align_bytes=64)
+                nc.scalar.copy(res[:, :, bcols], po[:])
+                if (c0 + w) % P == 0:
+                    scols = slice(c0 + w - P, c0 + w)
+                    nc.sync.dma_start(out_rows[:, :, scols], res[:, :, scols])
                 if b in CAST_ON_SCALAR:
-                    nc.scalar.copy(rb[:].rearrange("p (j t) -> p j t", t=PACK), po[:].rearrange("p t j -> p j t"))
-                else:
+                    nc.scalar.copy(rbs[b][:].rearrange("p (j t) -> p j t", t=PACK), po[:].rearrange("p t j -> p j t"))
+
+        def requantise(pieces):
+            for b, c0, w in pieces:
+                bcols = slice(c0, c0 + w)
+                if b not in CAST_ON_SCALAR:
                     nc.vector.tensor_copy(
-                        out=rb[:].rearrange("p (c i t) -> p c t i", t=PACK, i=2),
-                        in_=res[:].rearrange("p t (c i) -> p c t i", i=2),
+                        out=rbs[b][:].rearrange("p (c i t) -> p c t i", t=PACK, i=2),
+                        in_=res[:, :, bcols].rearrange("p t (c i) -> p c t i", i=2),
                     )
-                nc.vector.quantize_mx(out=ow[:, bcols].bitcast(FP8X4), scales=osc[:, bcols], in_=rb[:])
-                nc.sync.dma_start(out_words[:, bcols], ow[:, bcols].bitcast(I32))
+                nc.vector.quantize_mx(out=ow[:, bcols].bitcast(FP8X4), scales=osc[:, bcols], in_=rbs[b][:])
+            ccols = slice(pieces[0][1], pieces[-1][1] + pieces[-1][2])
+            nc.sync.dma_start(out_words[:, ccols], ow[:, ccols].bitcast(I32))
 
         start = 0
         pending = None
+        count = 0
         for ci, cw in enumerate(CHUNKS):
             cols = slice(start, start + cw)
             lcols = slice(start // 16, (start + cw) // 16)
@@ -172,31 +186,35 @@ def tile_picked_foodweb_none_po_kernel(
                         if u not in LC_ON_SCALAR:
                             nc.vector.tensor_copy(lc[u][:], pc[u][:])
                 nc.scalar.activation(c_food[t][:], lc[t][:].indirect(food_t[:, lcols]), ACT.Sigmoid)
-                if ci == 0:
-                    nc.scalar.activation(y[t][:], py[t][:], ACT.Sigmoid)
                 nc.scalar.activation(c_foe[t][:], lc[t][:].indirect(foe_t[:, lcols]), ACT.Sigmoid)
                 nc.vector.scalar_tensor_tensor(t1[:, t, :], c_food[t][:], 3.0, y[t][:, cols], ALU.mult, ALU.mult)
                 nc.vector.scalar_tensor_tensor(t2[:, t, :], c_foe[t][:], -2.0, t1[:, t, :], ALU.mult, ALU.add)
                 nc.vector.tensor_tensor(t3[:, t, :], y[t][:].indirect(own_t[:, lcols]), t2[:, t, :], ALU.add)
-                if ci == 0 and t in GY_ON_SCALAR:
-                    nc.scalar.activation(gy[:, t, :], y[t][:], ACT.Copy, scale=half_g[:, t : t + 1])
-                elif ci == 0:
-                    nc.vector.tensor_scalar(gy[:, t, :], y[t][:], half_g[:, t : t + 1], None, ALU.mult)
                 if ci == 0 and t == 0:
                     w3.extend([deal_words("dw3", w3w), deal_scales("ds3", w3s)])
                 if pending is not None and t == OUT_AFTER_TILE:
-                    finish(*pending)
-            zb = sb.tile([P, cw * PACK], BF16, name=f"zb{ci}", align_bytes=64)
-            nc.vector.tensor_tensor(
-                zb[:].rearrange("p (c i t) -> p c t i", t=PACK, i=2),
-                t3[:].rearrange("p t (c i) -> p c t i", i=2),
-                gy[:, :, cols].rearrange("p t (c i) -> p c t i", i=2),
-                ALU.mult,
-            )
-            nc.vector.quantize_mx(out=zw[:, cols].bitcast(FP8X4), scales=zs[:, cols], in_=zb[:])
-            pending = (start, cw)
+                    finish(pending)
+            pieces = []
+            c0 = start
+            for w in PIECES[ci]:
+                pcols = slice(c0, c0 + w)
+                zb = sb.tile([P, w * PACK], BF16, name=f"zb{count}", align_bytes=64)
+                nc.vector.tensor_tensor(
+                    zb[:].rearrange("p (c i t) -> p c t i", t=PACK, i=2),
+                    t3[:, :, c0 - start : c0 - start + w].rearrange("p t (c i) -> p c t i", i=2),
+                    gy[:, :, pcols].rearrange("p t (c i) -> p c t i", i=2),
+                    ALU.mult,
+                )
+                nc.vector.quantize_mx(out=zw[:, pcols].bitcast(FP8X4), scales=zs[:, pcols], in_=zb[:])
+                pieces.append((count, c0, w))
+                count += 1
+                c0 += w
+            if pending is not None:
+                requantise(pending)
+            pending = pieces
             start += cw
-        finish(*pending)
+        finish(pending)
+        requantise(pending)
         for q in range(4):
             eng = nc.sync if q % 2 == 0 else nc.scalar
             eng.dma_start(out_2[0][4 * q : 4 * q + 4, :].bitcast(I32), osc[32 * q : 32 * q + 4, :].bitcast(I32))

@@ -19,10 +19,10 @@ P = 128
 PACK = 4
 PIECES = ((128, 128), (64, 64, 64, 64))
 HALF = S // 2
-RING = 3
+RING = 4
 CHUNKS = (256, 256)
-LC_ON_SCALAR = (0,)
-CAST_ON_SCALAR = (0, 1, 2)
+LC_ON_SCALAR = (0, 1)
+CAST_ON_SCALAR = (0, 1)
 OUT_AFTER_TILE = 3
 
 
@@ -45,10 +45,10 @@ def tile_picked_foodweb_none_po_kernel(
             nc.sync.dma_start(t[:].bitcast(I32), src[0].rearrange("p n t -> p (n t)").bitcast(I32))
             return t
 
-        def load_scales(dst, src, first=0, quads=range(4)):
+        def load_scales(dst, src, first=0, quads=range(4), queues=(nc.sync,)):
             for q in quads:
                 r = 32 * q + first
-                nc.sync.dma_start(dst[r : r + 4, :].bitcast(I32), src[0][4 * q : 4 * q + 4, :].bitcast(I32))
+                queues[q % len(queues)].dma_start(dst[r : r + 4, :].bitcast(I32), src[0][4 * q : 4 * q + 4, :].bitcast(I32))
 
         def deal_words(name, words):
             dw = sb.tile([P, H], I32, name=name, align_bytes=64)
@@ -76,9 +76,10 @@ def tile_picked_foodweb_none_po_kernel(
         xs = sb.tile([P, T], U8, name="xs", align_bytes=64)
         nc.vector.memset(xs[:].bitcast(I32), 0)
         w12s = sb.tile([P, H], U8, name="w12s", tag="raw_then_picked", align_bytes=64)
+        w2s = sb.tile([P, H], U8, name="w2s", align_bytes=64)
         w3s = sb.tile([P, N], U8, name="w3s", align_bytes=64)
         zs = sb.tile([P, S], U8, name="zs", align_bytes=64)
-        for t_ in (w12s, w3s):
+        for t_ in (w12s, w2s, w3s):
             nc.vector.memset(t_[:].bitcast(I32), 0)
 
         warm = sb.tile([P, 2], F32, name="warm")
@@ -86,14 +87,13 @@ def tile_picked_foodweb_none_po_kernel(
         nc.scalar.activation(warm[:, 1:2], warm[:, 0:1], ACT.Sigmoid)
 
         offs_t = load_list("offs_t", offs)
-        two_t = load_list("two_t", two)
         w1w = load_words("w1w", w1_words, H)
-        w2w = load_words("w2w", w2_words, H)
-        load_scales(xs, x_scales)
-        load_scales(w12s, w1_scales, 0, range(0, 1))
+        two_t = load_list("two_t", two)
+        load_scales(xs, x_scales, queues=(nc.sync,))
         xw = load_words("xw", x_words, T)
-        load_scales(w12s, w1_scales, 0, range(1, 4))
-        load_scales(w12s, w2_scales, 4)
+        load_scales(w12s, w1_scales)
+        w2w = load_words("w2w", w2_words, H)
+        load_scales(w2s, w2_scales)
         food_t = load_list("food_t", food)
         foe_t = load_list("foe_t", foe)
         g = sb.tile([P, PACK], F32, name="g")
@@ -103,7 +103,6 @@ def tile_picked_foodweb_none_po_kernel(
         load_scales(w3s, w3_scales)
 
         dw1 = deal_words("dw1", w1w)
-        dw2 = deal_words("dw2", w2w)
         xs1 = sb.tile([P, S], U8, name="xs1", align_bytes=64)
         nc.vector.tensor_copy(xs1[:], xs[:].indirect(offs_t[:]))
         xs2 = sb.tile([P, S], U8, name="xs2", align_bytes=64)
@@ -123,9 +122,11 @@ def tile_picked_foodweb_none_po_kernel(
                 nc.scalar.activation(y[t][:, hc], py[t][:, hc], ACT.Sigmoid)
         xw2 = later[:, HALF:]
         nc.vector.tensor_copy(xw2, xw[:].indirect(two_t[:]))
+        dw2 = deal_words("dw2", w2w)
+        ds2 = deal_scales("ds2", w2s)
         pc = [psum.tile([P, S], F32, name=f"pc{t}", tag=f"bank{PACK + t}") for t in range(PACK)]
         for t in range(PACK):
-            product(pc[t][:], dw2, ds12, 4, t, xw2, xs2[:])
+            product(pc[t][:], dw2, ds2, 0, t, xw2, xs2[:])
 
         lc = [sb.tile([P, S], F32, name=f"lc{t}") for t in range(PACK)]
         gy = sb.tile([P, PACK, S], F32, name="gy")
@@ -149,8 +150,8 @@ def tile_picked_foodweb_none_po_kernel(
                     product(po[:, t, :], w3[0], w3[1], 0, t, zw[:, bcols], zs[:, bcols])
                 rbs[b] = sb.tile([P, w * PACK], BF16, name=f"rb{b}", align_bytes=64)
                 nc.scalar.copy(res[:, :, bcols], po[:])
-                if (c0 + w) % P == 0:
-                    scols = slice(c0 + w - P, c0 + w)
+                if (c0 + w) % P == 0 or c0 >= S - P:
+                    scols = bcols if c0 >= S - P else slice(c0 + w - P, c0 + w)
                     nc.sync.dma_start(out_rows[:, :, scols], res[:, :, scols])
                 if b in CAST_ON_SCALAR:
                     nc.scalar.copy(rbs[b][:].rearrange("p (j t) -> p j t", t=PACK), po[:].rearrange("p t j -> p j t"))

@@ -19,10 +19,10 @@ P = 128
 PACK = 4
 PIECES = ((128, 128), (64, 64, 64, 64))
 HALF = S // 2
-RING = 4
+RING = 3
 CHUNKS = (256, 256)
-LC_ON_SCALAR = (0, 1)
-CAST_ON_SCALAR = (0, 1)
+LC_ON_SCALAR = (0,)
+CAST_ON_SCALAR = (0, 1, 2)
 OUT_AFTER_TILE = 3
 
 
@@ -150,8 +150,8 @@ def tile_picked_foodweb_none_po_kernel(
                     product(po[:, t, :], w3[0], w3[1], 0, t, zw[:, bcols], zs[:, bcols])
                 rbs[b] = sb.tile([P, w * PACK], BF16, name=f"rb{b}", align_bytes=64)
                 nc.scalar.copy(res[:, :, bcols], po[:])
-                if (c0 + w) % P == 0 or c0 >= S - P:
-                    scols = bcols if c0 >= S - P else slice(c0 + w - P, c0 + w)
+                if (c0 + w) % P == 0:
+                    scols = slice(c0 + w - P, c0 + w)
                     nc.sync.dma_start(out_rows[:, :, scols], res[:, :, scols])
                 if b in CAST_ON_SCALAR:
                     nc.scalar.copy(rbs[b][:].rearrange("p (j t) -> p j t", t=PACK), po[:].rearrange("p t j -> p j t"))

from contextlib import ExitStack

import concourse.mybir as mybir

K, T, S, N, H = 512, 2048, 512, 512, 512
FLOPS = 2 * K * H * S * 2 + 2 * H * N * S

F32 = mybir.dt.float32
BF16 = mybir.dt.bfloat16
I32 = mybir.dt.int32
U32 = mybir.dt.uint32
U16 = mybir.dt.uint16
U8 = mybir.dt.uint8
FP8X4 = mybir.dt.float8_e4m3fn_x4
ALU = mybir.AluOpType
ACT = mybir.ActivationFunctionType

P = 128
PACK = 4
PIECES = ((128, 128), (64, 64, 64, 64))
HALF = S // 2
RING = 3
CHUNKS = (256, 256)
LC_ON_SCALAR = (0,)
CAST_ON_SCALAR = (0, 1, 2)
OUT_AFTER_TILE = 3


def tile_picked_foodweb_none_po_kernel(
    tc, x_words, x_scales, w1_words, w1_scales, w2_words, w2_scales, gn, w3_words, w3_scales,
    offs, two, own_l, foe, food, out_0, out_1, out_2,
):
    nc = tc.nc
    with ExitStack() as ctx:
        sb = ctx.enter_context(tc.tile_pool(name="sb", bufs=1))
        psum = ctx.enter_context(tc.psum_pool(name="psum", bufs=1))

        def load_list(name, src):
            t = sb.tile([P, S // 16], U16, name=name)
            nc.sync.dma_start(t[:], src)
            return t

        def load_words(name, src, width):
            t = sb.tile([P, width], U32, name=name, align_bytes=64)
            nc.sync.dma_start(t[:].bitcast(I32), src[0].rearrange("p n t -> p (n t)").bitcast(I32))
            return t

        def load_scales(dst, src, first=0, quads=range(4), queues=(nc.sync,)):
            for q in quads:
                r = 32 * q + first
                queues[q % len(queues)].dma_start(dst[r : r + 4, :].bitcast(I32), src[0][4 * q : 4 * q + 4, :].bitcast(I32))

        def deal_words(name, words):
            dw = sb.tile([P, H], I32, name=name, align_bytes=64)
            nc.vector.tensor_copy(
                out=dw[:].rearrange("p (t c i) -> p c t i", t=PACK, i=4),
                in_=words[:].bitcast(I32).rearrange("p (c i t) -> p c t i", t=PACK, i=4),
            )
            return dw

        def deal_scales(name, scales):
            ds = sb.tile([P, H], U8, name=name, align_bytes=64)
            nc.vector.tensor_copy(
                out=ds[:].rearrange("p (t c i) -> p c t i", t=PACK, i=16),
                in_=scales[:].rearrange("p (c i t) -> p c t i", t=PACK, i=16),
            )
            return ds

        def product(bank, dw, ds, first, t, words, scales):
            cols = slice(P * t, P * (t + 1))
            nc.tensor.matmul_mx(
                out=bank, lhsT=dw[:, cols].bitcast(FP8X4), lhsT_scale=ds[first:P, cols],
                rhs=words.bitcast(FP8X4), rhs_scale=scales, start=True, stop=True,
            )

        xs = sb.tile([P, T], U8, name="xs", align_bytes=64)
        nc.vector.memset(xs[:].bitcast(I32), 0)
        w12s = sb.tile([P, H], U8, name="w12s", tag="raw_then_picked", align_bytes=64)
        w2s = sb.tile([P, H], U8, name="w2s", align_bytes=64)
        w3s = sb.tile([P, N], U8, name="w3s", align_bytes=64)
        zs = sb.tile([P, S], U8, name="zs", align_bytes=64)
        for t_ in (w12s, w2s, w3s):
            nc.vector.memset(t_[:].bitcast(I32), 0)

        warm = sb.tile([P, 2], F32, name="warm")
        nc.vector.memset(warm[:, 0:1], 0.0)
        nc.scalar.activation(warm[:, 1:2], warm[:, 0:1], ACT.Sigmoid)

        offs_t = load_list("offs_t", offs)
        w1w = load_words("w1w", w1_words, H)
        two_t = load_list("two_t", two)
        load_scales(xs, x_scales, queues=(nc.sync,))
        xw = load_words("xw", x_words, T)
        load_scales(w12s, w1_scales)
        w2w = load_words("w2w", w2_words, H)
        load_scales(w2s, w2_scales)
        food_t = load_list("food_t", food)
        foe_t = load_list("foe_t", foe)
        g = sb.tile([P, PACK], F32, name="g")
        nc.sync.dma_start(g[:], gn.rearrange("(p t) o -> p (t o)", t=PACK))
        own_t = load_list("own_t", own_l)
        w3w = load_words("w3w", w3_words, N)
        load_scales(w3s, w3_scales)

        dw1 = deal_words("dw1", w1w)
        xs1 = sb.tile([P, S], U8, name="xs1", align_bytes=64)
        nc.vector.tensor_copy(xs1[:], xs[:].indirect(offs_t[:]))
        xs2 = sb.tile([P, S], U8, name="xs2", align_bytes=64)
        nc.vector.tensor_copy(xs2[:], xs[:].indirect(two_t[:]))
        y = [sb.tile([P, S], F32, name=f"y{t}") for t in range(PACK)]
        py = [psum.tile([P, S], F32, name=f"py{t}", tag=f"bank{t}") for t in range(PACK)]
        xw1_first = sb.tile([P, HALF], U32, name="xw1_first", align_bytes=64)
        nc.vector.tensor_copy(xw1_first[:], xw[:].indirect(offs_t[:, : HALF // 16]))
        ds12 = deal_scales("ds12", w12s)
        later = sb.tile([P, HALF + S], U32, name="later", tag="raw_then_picked", align_bytes=64)
        nc.vector.tensor_copy(later[:, :HALF], xw[:].indirect(offs_t[:, HALF // 16 :]))
        for a, xw1 in enumerate((xw1_first[:], later[:, :HALF])):
            hc = slice(a * HALF, (a + 1) * HALF)
            for t in range(PACK):
                product(py[t][:, hc], dw1, ds12, 0, t, xw1, xs1[:, hc])
            for t in range(PACK):
                nc.scalar.activation(y[t][:, hc], py[t][:, hc], ACT.Sigmoid)
        xw2 = later[:, HALF:]
        nc.vector.tensor_copy(xw2, xw[:].indirect(two_t[:]))
        dw2 = deal_words("dw2", w2w)
        ds2 = deal_scales("ds2", w2s)
        pc = [psum.tile([P, S], F32, name=f"pc{t}", tag=f"bank{PACK + t}") for t in range(PACK)]
        for t in range(PACK):
            product(pc[t][:], dw2, ds2, 0, t, xw2, xs2[:])

        lc = [sb.tile([P, S], F32, name=f"lc{t}") for t in range(PACK)]
        gy = sb.tile([P, PACK, S], F32, name="gy")
        osc = sb.tile([P, S], U8, name="osc", align_bytes=64)
        ow = sb.tile([P, S], U32, name="ow", align_bytes=64)
        zw = sb.tile([P, S], U32, name="zw", align_bytes=64)
        out_rows = out_0.rearrange("(p t) j -> p t j", t=PACK)
        out_words = out_1[0].rearrange("p n t -> p (n t)").bitcast(I32)
        w3 = []
        for t in range(PACK):
            nc.vector.tensor_scalar(gy[:, t, :], y[t][:], g[:, t : t + 1], 0.5, ALU.mult, ALU.mult)

        res = sb.tile([P, PACK, S], F32, name="res")
        rbs = {}

        def finish(pieces):
            for b, c0, w in pieces:
                bcols = slice(c0, c0 + w)
                po = psum.tile([P, PACK, w], F32, name=f"po{b}", tag=f"bank{b % PACK}")
                for t in range(PACK):
                    product(po[:, t, :], w3[0], w3[1], 0, t, zw[:, bcols], zs[:, bcols])
                rbs[b] = sb.tile([P, w * PACK], BF16, name=f"rb{b}", align_bytes=64)
                nc.scalar.copy(res[:, :, bcols], po[:])
                if (c0 + w) % P == 0:
                    scols = slice(c0 + w - P, c0 + w)
                    nc.sync.dma_start(out_rows[:, :, scols], res[:, :, scols])
                if b in CAST_ON_SCALAR:
                    nc.scalar.copy(rbs[b][:].rearrange("p (j t) -> p j t", t=PACK), po[:].rearrange("p t j -> p j t"))

        def requantise(pieces):
            for b, c0, w in pieces:
                bcols = slice(c0, c0 + w)
                if b not in CAST_ON_SCALAR:
                    nc.vector.tensor_copy(
                        out=rbs[b][:].rearrange("p (c i t) -> p c t i", t=PACK, i=2),
                        in_=res[:, :, bcols].rearrange("p t (c i) -> p c t i", i=2),
                    )
                nc.vector.quantize_mx(out=ow[:, bcols].bitcast(FP8X4), scales=osc[:, bcols], in_=rbs[b][:])
            ccols = slice(pieces[0][1], pieces[-1][1] + pieces[-1][2])
            nc.sync.dma_start(out_words[:, ccols], ow[:, ccols].bitcast(I32))

        start = 0
        pending = None
        count = 0
        for ci, cw in enumerate(CHUNKS):
            cols = slice(start, start + cw)
            lcols = slice(start // 16, (start + cw) // 16)
            c_food = [sb.tile([P, cw], F32, name=f"c_food{ci}_{t}", tag="c_food", bufs=RING) for t in range(PACK)]
            c_foe = [sb.tile([P, cw], F32, name=f"c_foe{ci}_{t}", tag="c_foe", bufs=RING) for t in range(PACK)]
            t1 = sb.tile([P, PACK, cw], F32, name=f"t1_{ci}")
            t2 = sb.tile([P, PACK, cw], F32, name=f"t2_{ci}")
            t3 = sb.tile([P, PACK, cw], F32, name=f"t3_{ci}")
            for t in range(PACK):
                if ci == 0 and t in LC_ON_SCALAR:
                    nc.scalar.copy(lc[t][:], pc[t][:])
                if ci == 0 and t == 0:
                    for u in range(PACK):
                        if u not in LC_ON_SCALAR:
                            nc.vector.tensor_copy(lc[u][:], pc[u][:])
                nc.scalar.activation(c_food[t][:], lc[t][:].indirect(food_t[:, lcols]), ACT.Sigmoid)
                nc.scalar.activation(c_foe[t][:], lc[t][:].indirect(foe_t[:, lcols]), ACT.Sigmoid)
                nc.vector.scalar_tensor_tensor(t1[:, t, :], c_food[t][:], 3.0, y[t][:, cols], ALU.mult, ALU.mult)
                nc.vector.scalar_tensor_tensor(t2[:, t, :], c_foe[t][:], -2.0, t1[:, t, :], ALU.mult, ALU.add)
                nc.vector.tensor_tensor(t3[:, t, :], y[t][:].indirect(own_t[:, lcols]), t2[:, t, :], ALU.add)
                if ci == 0 and t == 0:
                    w3.extend([deal_words("dw3", w3w), deal_scales("ds3", w3s)])
                if pending is not None and t == OUT_AFTER_TILE:
                    finish(pending)
            pieces = []
            c0 = start
            for w in PIECES[ci]:
                pcols = slice(c0, c0 + w)
                zb = sb.tile([P, w * PACK], BF16, name=f"zb{count}", align_bytes=64)
                nc.vector.tensor_tensor(
                    zb[:].rearrange("p (c i t) -> p c t i", t=PACK, i=2),
                    t3[:, :, c0 - start : c0 - start + w].rearrange("p t (c i) -> p c t i", i=2),
                    gy[:, :, pcols].rearrange("p t (c i) -> p c t i", i=2),
                    ALU.mult,
                )
                nc.vector.quantize_mx(out=zw[:, pcols].bitcast(FP8X4), scales=zs[:, pcols], in_=zb[:])
                pieces.append((count, c0, w))
                count += 1
                c0 += w
            if pending is not None:
                requantise(pending)
            pending = pieces
            start += cw
        finish(pending)
        requantise(pending)
        for q in range(4):
            eng = nc.sync if q % 2 == 0 else nc.scalar
            eng.dma_start(out_2[0][4 * q : 4 * q + 4, :].bitcast(I32), osc[32 * q : 32 * q + 4, :].bitcast(I32))
